import numpy as np, ml_dtypes
CORES = [2,10,50,58,66,74,122]
N = 7
R = 32
def setup_inputs(rng):
    m = (rng.standard_normal((N, 128, 128), dtype=np.float32) / 11).astype(ml_dtypes.bfloat16)
    q = rng.standard_normal((128, R), dtype=np.float32).astype(ml_dtypes.bfloat16)
    return {"m": m, "mt": m.transpose(0, 2, 1).copy(), "q": np.broadcast_to(q, (N, 128, R)).copy()}
def setup_inputs_big(rng):
    d = setup_inputs(rng)
    for k in ("m", "mt", "q"): d[k] = (d[k].astype(np.float32) * 1024.0).astype(d[k].dtype)
    return d
def setup_inputs_small(rng):
    d = setup_inputs(rng)
    for k in ("m", "mt", "q"): d[k] = (d[k].astype(np.float32) * (1 / 1024.0)).astype(d[k].dtype)
    return d
def setup_inputs_apart(rng):
    d = setup_inputs(rng)
    f = (10.0 ** rng.permutation(np.linspace(-1.5, 1.5, N))).astype(np.float32).reshape(N, 1, 1)
    for k in ("m", "mt"): d[k] = (d[k].astype(np.float32) * f).astype(d[k].dtype)
    return d
def tie_inputs(x):
    x = dict(x)
    x["mt"] = x["m"].transpose(0, 2, 1).copy(); x["q"] = np.broadcast_to(x["q"][0], x["q"].shape).copy()
    return x
def reference(m, mt, q):
    M, MT, Q = m.astype(np.float64), mt.astype(np.float64), q.astype(np.float64)
    p = sum(MT[j].T @ Q[j] for j in range(N))
    q2 = sum(M[j].T @ p for j in range(N))
    return {"p": np.broadcast_to(p.astype(ml_dtypes.bfloat16 if m.dtype != np.float64 else np.float64), (N, 128, R)), "q2": np.broadcast_to(q2.astype(ml_dtypes.bfloat16 if m.dtype != np.float64 else np.float64), (N, 128, R))}

@@ -1,0 +1,92 @@
+from concourse.bass import DstId, RemoteDMATransfer
+from concourse.mybir import AluOpType
+
+N = 7
+D = 128
+R = 32
+W = D + R
+
+SCRATCH = {
+    "land": ("sbuf", [128, N * W], "bfloat16"),
+    "mts": ("sbuf", [128, D], "bfloat16"),
+    "qs": ("sbuf", [128, R], "bfloat16"),
+    "acc": ("sbuf", [128, (N - 2) * R], "float32"),
+    "pf": ("sbuf", [128, R], "bfloat16"),
+    "q2s": ("sbuf", [128, R], "bfloat16"),
+    "pp": ("psum", [128, 512], "float32"),
+    "pq": ("psum", [128, 512], "float32"),
+}
+SEMAPHORES = ["ld", "ldm", "mm1", "pj", "vs", "mm2", "q2c", "st", "sent"] + ["a%d" % j for j in range(N)]
+
+
+def rank_program(g, core, T, topo):
+    r = T.rank_of(core)
+    if r is None:
+        return
+    S = T.sem
+    cores = T.cores
+
+    def m_of(j):
+        return T.land[:, j * W:j * W + D]
+
+    def p_of(j):
+        return T.land[:, j * W + D:(j + 1) * W]
+
+    def slot(j):
+        return T.land[:, j * W:(j + 1) * W]
+
+    g.sync.dma_start(T.mts[:, :], T.mt[:, :]).then_inc(S.ld, 16)
+    g.scalar.dma_start(T.qs[:, :], T.q[:, :]).then_inc(S.ld, 16)
+    g.scalar.dma_start(m_of(r), T.m[:, :]).then_inc(S.ldm, 16)
+
+    g.tensor.wait_ge(S.ld, 32)
+    g.tensor.matmul(T.pp[:, 0:R], T.mts[:, :], T.qs[:, :], start=True, stop=True).then_inc(S.mm1, 1)
+    g.vector.wait_ge(S.mm1, 1)
+    g.vector.tensor_copy(p_of(r), T.pp[:, 0:R]).then_inc(S.pj, 1)
+
+    dsts = [cores[(r + k) % N] for k in range(1, N)]
+    mask = topo.mask(core, dsts[0])
+    for d in dsts:
+        if not topo.may_write(core, d):
+            raise ValueError("core %d may not write to core %d" % (core, d))
+        mask &= topo.mask(core, d)
+    n_eng = bin(mask).count("1")
+    ids = []
+    for d in dsts:
+        rid, pid, _se = topo.addr(d)
+        ids.append(DstId(rid=rid, pnc=pid))
+    g.wait_ge(S.pj, 1)
+    g.wait_ge(S.ldm, 16)
+    g.remote_dma_fused(
+        [RemoteDMATransfer(dst_ids=ids, dma_engine_mask=mask, remote_sem=S["a%d" % r],
+                           srcs=[slot(r)], dsts=[slot(r) for _d in dsts], alu_op=0)],
+        local_sem=S.sent)
+
+    order = [(r - k) % N for k in range(1, N)]
+    prev = T.pp[:, 0:R]
+    for k, j in enumerate(order):
+        out = T.pf[:, :] if k == N - 2 else T.acc[:, k * R:(k + 1) * R]
+        g.vector.wait_ge(S["a%d" % j], n_eng)
+        if k:
+            g.vector.wait_ge(S.vs, k)
+        g.vector.tensor_tensor(out, prev, p_of(j), AluOpType.add).then_inc(S.vs, 1)
+        prev = out
+
+    g.scalar.wait_ge(S.vs, N - 1)
+    g.scalar.dma_start(T.p[:, :], T.pf[:, :]).then_inc(S.st, 16)
+
+    g.tensor.wait_ge(S.ldm, 16)
+    for j in order:
+        g.tensor.wait_ge(S["a%d" % j], n_eng)
+    g.tensor.wait_ge(S.vs, N - 1)
+    seq = [r] + order
+    for k, j in enumerate(seq):
+        mm = g.tensor.matmul(T.pq[:, 0:R], m_of(j), T.pf[:, :], start=(k == 0), stop=(k == N - 1))
+    mm.then_inc(S.mm2, 1)
+    g.vector.wait_ge(S.mm2, 1)
+    g.vector.tensor_copy(T.q2s[:, :], T.pq[:, 0:R]).then_inc(S.q2c, 1)
+    g.sync.wait_ge(S.q2c, 1)
+    g.sync.dma_start(T.q2[:, :], T.q2s[:, :]).then_inc(S.st, 16)
+
+    g.wait_ge(S.sent, n_eng)
+    g.wait_ge(S.st, 32)

@@ -1,22 +1,24 @@
 from concourse.bass import DstId, RemoteDMATransfer
-from concourse.mybir import AluOpType
+from concourse.mybir import AluOpType, ActivationFunctionType
 
 N = 7
 D = 128
 R = 32
-W = D + R
 
 SCRATCH = {
-    "land": ("sbuf", [128, N * W], "bfloat16"),
-    "mts": ("sbuf", [128, D], "bfloat16"),
+    "land": ("sbuf", [128, N * D], "bfloat16"),
     "qs": ("sbuf", [128, R], "bfloat16"),
-    "acc": ("sbuf", [128, (N - 2) * R], "float32"),
+    "ones": ("sbuf", [128, D], "bfloat16"),
+    "idn": ("sbuf", [128, D], "bfloat16"),
+    "ms": ("sbuf", [128, D], "bfloat16"),
     "pf": ("sbuf", [128, R], "bfloat16"),
     "q2s": ("sbuf", [128, R], "bfloat16"),
+    "pm": ("psum", [128, 512], "float32"),
     "pp": ("psum", [128, 512], "float32"),
     "pq": ("psum", [128, 512], "float32"),
 }
-SEMAPHORES = ["ld", "ldm", "mm1", "pj", "vs", "mm2", "q2c", "st", "sent"] + ["a%d" % j for j in range(N)]
+SEMAPHORES = ["ld", "ldq", "on", "idy", "tm", "tp", "mc", "pc", "mm2", "q2c", "st", "sent"] + \
+             ["a%d" % j for j in range(N)]
 
 
 def rank_program(g, core, T, topo):
@@ -26,23 +28,12 @@ def rank_program(g, core, T, topo):
     S = T.sem
     cores = T.cores
 
-    def m_of(j):
-        return T.land[:, j * W:j * W + D]
-
-    def p_of(j):
-        return T.land[:, j * W + D:(j + 1) * W]
-
     def slot(j):
-        return T.land[:, j * W:(j + 1) * W]
+        return T.land[:, j * D:(j + 1) * D]
 
-    g.sync.dma_start(T.mts[:, :], T.mt[:, :]).then_inc(S.ld, 16)
-    g.scalar.dma_start(T.qs[:, :], T.q[:, :]).then_inc(S.ld, 16)
-    g.scalar.dma_start(m_of(r), T.m[:, :]).then_inc(S.ldm, 16)
-
-    g.tensor.wait_ge(S.ld, 32)
-    g.tensor.matmul(T.pp[:, 0:R], T.mts[:, :], T.qs[:, :], start=True, stop=True).then_inc(S.mm1, 1)
-    g.vector.wait_ge(S.mm1, 1)
-    g.vector.tensor_copy(p_of(r), T.pp[:, 0:R]).then_inc(S.pj, 1)
+    g.sync.dma_start(slot(r), T.mt[:, :]).then_inc(S.ld, 16)
+    g.scalar.dma_start(T.qs[:, :], T.q[:, :]).then_inc(S.ldq, 16)
+    g.vector.memset(T.ones[:, :], 1.0).then_inc(S.on, 1)
 
     dsts = [cores[(r + k) % N] for k in range(1, N)]
     mask = topo.mask(core, dsts[0])
@@ -55,34 +46,39 @@ def rank_program(g, core, T, topo):
     for d in dsts:
         rid, pid, _se = topo.addr(d)
         ids.append(DstId(rid=rid, pnc=pid))
-    g.wait_ge(S.pj, 1)
-    g.wait_ge(S.ldm, 16)
+    g.wait_ge(S.ld, 16)
     g.remote_dma_fused(
         [RemoteDMATransfer(dst_ids=ids, dma_engine_mask=mask, remote_sem=S["a%d" % r],
                            srcs=[slot(r)], dsts=[slot(r) for _d in dsts], alu_op=0)],
         local_sem=S.sent)
 
-    order = [(r - k) % N for k in range(1, N)]
-    prev = T.pp[:, 0:R]
-    for k, j in enumerate(order):
-        out = T.pf[:, :] if k == N - 2 else T.acc[:, k * R:(k + 1) * R]
-        g.vector.wait_ge(S["a%d" % j], n_eng)
-        if k:
-            g.vector.wait_ge(S.vs, k)
-        g.vector.tensor_tensor(out, prev, p_of(j), AluOpType.add).then_inc(S.vs, 1)
-        prev = out
+    g.wait_ge(S.on, 1)
+    g.affine_select(T.idn[:, :], T.ones[:, :], [[-1, D]], AluOpType.is_equal, 0.0, 0, 1).then_inc(S.idy, 1)
 
-    g.scalar.wait_ge(S.vs, N - 1)
+    order = [(r - k) % N for k in range(1, N)]
+    seq = [r] + order
+    g.tensor.wait_ge(S.ld, 16)
+    g.tensor.wait_ge(S.ldq, 16)
+    g.tensor.wait_ge(S.idy, 1)
+    for k, j in enumerate(seq):
+        if k:
+            g.tensor.wait_ge(S["a%d" % j], n_eng)
+        first, last = (k == 0), (k == N - 1)
+        mm_m = g.tensor.matmul(T.pm[:, 0:D], slot(j), T.idn[:, :], start=first, stop=last)
+        mm_p = g.tensor.matmul(T.pp[:, 0:R], slot(j), T.qs[:, :], start=first, stop=last)
+    mm_m.then_inc(S.tm, 1)
+    mm_p.then_inc(S.tp, 1)
+
+    g.vector.wait_ge(S.tm, 1)
+    g.vector.tensor_copy(T.ms[:, :], T.pm[:, 0:D]).then_inc(S.mc, 1)
+    g.scalar.wait_ge(S.tp, 1)
+    g.scalar.activation(T.pf[:, :], T.pp[:, 0:R], ActivationFunctionType.Copy).then_inc(S.pc, 1)
+    g.scalar.wait_ge(S.pc, 1)
     g.scalar.dma_start(T.p[:, :], T.pf[:, :]).then_inc(S.st, 16)
 
-    g.tensor.wait_ge(S.ldm, 16)
-    for j in order:
-        g.tensor.wait_ge(S["a%d" % j], n_eng)
-    g.tensor.wait_ge(S.vs, N - 1)
-    seq = [r] + order
-    for k, j in enumerate(seq):
-        mm = g.tensor.matmul(T.pq[:, 0:R], m_of(j), T.pf[:, :], start=(k == 0), stop=(k == N - 1))
-    mm.then_inc(S.mm2, 1)
+    g.tensor.wait_ge(S.mc, 1)
+    g.tensor.wait_ge(S.pc, 1)
+    g.tensor.matmul(T.pq[:, 0:R], T.ms[:, :], T.pf[:, :], start=True, stop=True).then_inc(S.mm2, 1)
     g.vector.wait_ge(S.mm2, 1)
     g.vector.tensor_copy(T.q2s[:, :], T.pq[:, 0:R]).then_inc(S.q2c, 1)
     g.sync.wait_ge(S.q2c, 1)

@@ -4,20 +4,23 @@ from concourse.mybir import AluOpType, ActivationFunctionType
 N = 7
 D = 128
 R = 32
+W = D + R
+NP = 4
 
 SCRATCH = {
-    "land": ("sbuf", [128, N * D], "bfloat16"),
-    "qs": ("sbuf", [128, R], "bfloat16"),
+    "landp": ("sbuf", [128, (NP + 1) * D], "bfloat16"),
+    "landq": ("sbuf", [128, (N - 1 - NP) * W], "bfloat16"),
+    "snd": ("sbuf", [128, W], "bfloat16"),
+    "iq": ("sbuf", [128, W], "bfloat16"),
     "ones": ("sbuf", [128, D], "bfloat16"),
-    "idn": ("sbuf", [128, D], "bfloat16"),
-    "ms": ("sbuf", [128, D], "bfloat16"),
+    "asum": ("sbuf", [128, W], "bfloat16"),
     "pf": ("sbuf", [128, R], "bfloat16"),
     "q2s": ("sbuf", [128, R], "bfloat16"),
-    "pm": ("psum", [128, 512], "float32"),
-    "pp": ("psum", [128, 512], "float32"),
+    "pa": ("psum", [128, 512], "float32"),
+    "pj": ("psum", [128, 512], "float32"),
     "pq": ("psum", [128, 512], "float32"),
 }
-SEMAPHORES = ["ld", "ldq", "on", "idy", "tm", "tp", "mc", "pc", "mm2", "q2c", "st", "sent"] + \
+SEMAPHORES = ["ld", "ldm", "ldq", "on", "idy", "tj", "sj", "tm", "mc", "pc", "mm2", "q2c", "st", "sent"] + \
              ["a%d" % j for j in range(N)]
 
 
@@ -28,61 +31,83 @@ def rank_program(g, core, T, topo):
     S = T.sem
     cores = T.cores
 
-    def slot(j):
-        return T.land[:, j * D:(j + 1) * D]
+    def slotp(k):
+        return T.landp[:, k * D:(k + 1) * D]
 
-    g.sync.dma_start(slot(r), T.mt[:, :]).then_inc(S.ld, 16)
-    g.scalar.dma_start(T.qs[:, :], T.q[:, :]).then_inc(S.ldq, 16)
+    def slotq(k, lo=0, hi=W):
+        base = (k - NP - 1) * W
+        return T.landq[:, base + lo:base + hi]
+
+    def arr(k):
+        return S["a%d" % ((r - k) % N)]
+
+    g.sync.dma_start(slotp(0), T.mt[:, :]).then_inc(S.ld, 16)
+    g.scalar.dma_start(T.iq[:, D:W], T.q[:, :]).then_inc(S.ldq, 16)
+    g.sync.dma_start(T.snd[:, 0:D], T.m[:, :]).then_inc(S.ldm, 16)
     g.vector.memset(T.ones[:, :], 1.0).then_inc(S.on, 1)
 
     dsts = [cores[(r + k) % N] for k in range(1, N)]
     mask = topo.mask(core, dsts[0])
+    ids = []
     for d in dsts:
         if not topo.may_write(core, d):
             raise ValueError("core %d may not write to core %d" % (core, d))
         mask &= topo.mask(core, d)
-    n_eng = bin(mask).count("1")
-    ids = []
-    for d in dsts:
         rid, pid, _se = topo.addr(d)
         ids.append(DstId(rid=rid, pnc=pid))
+    n_eng = bin(mask).count("1")
+
     g.wait_ge(S.ld, 16)
     g.remote_dma_fused(
-        [RemoteDMATransfer(dst_ids=ids, dma_engine_mask=mask, remote_sem=S["a%d" % r],
-                           srcs=[slot(r)], dsts=[slot(r) for _d in dsts], alu_op=0)],
+        [RemoteDMATransfer(dst_ids=ids[0:NP], dma_engine_mask=mask, remote_sem=S["a%d" % r],
+                           srcs=[slotp(0)], dsts=[slotp(k) for k in range(1, NP + 1)], alu_op=0)],
         local_sem=S.sent)
 
     g.wait_ge(S.on, 1)
-    g.affine_select(T.idn[:, :], T.ones[:, :], [[-1, D]], AluOpType.is_equal, 0.0, 0, 1).then_inc(S.idy, 1)
+    g.affine_select(T.iq[:, 0:D], T.ones[:, :], [[-1, D]], AluOpType.is_equal, 0.0, 0, 1).then_inc(S.idy, 1)
 
-    order = [(r - k) % N for k in range(1, N)]
-    seq = [r] + order
     g.tensor.wait_ge(S.ld, 16)
     g.tensor.wait_ge(S.ldq, 16)
-    g.tensor.wait_ge(S.idy, 1)
-    for k, j in enumerate(seq):
-        if k:
-            g.tensor.wait_ge(S["a%d" % j], n_eng)
-        first, last = (k == 0), (k == N - 1)
-        mm_m = g.tensor.matmul(T.pm[:, 0:D], slot(j), T.idn[:, :], start=first, stop=last)
-        mm_p = g.tensor.matmul(T.pp[:, 0:R], slot(j), T.qs[:, :], start=first, stop=last)
-    mm_m.then_inc(S.tm, 1)
-    mm_p.then_inc(S.tp, 1)
+    g.tensor.matmul(T.pj[:, 0:R], slotp(0), T.iq[:, D:W], start=True, stop=True).then_inc(S.tj, 1)
+    g.scalar.wait_ge(S.tj, 1)
+    g.scalar.activation(T.snd[:, D:W], T.pj[:, 0:R], ActivationFunctionType.Copy).then_inc(S.sj, 1)
 
+    g.wait_ge(S.sj, 1)
+    g.wait_ge(S.ldm, 16)
+    g.remote_dma_fused(
+        [RemoteDMATransfer(dst_ids=ids[NP:], dma_engine_mask=mask, remote_sem=S["a%d" % r],
+                           srcs=[T.snd[:, :]], dsts=[slotq(k) for k in range(NP + 1, N)], alu_op=0)],
+        local_sem=S.sent)
+
+    g.tensor.wait_ge(S.idy, 1)
+    for k in range(NP + 1):
+        if k:
+            g.tensor.wait_ge(arr(k), n_eng)
+        mm = g.tensor.matmul(T.pa[:, 0:W], slotp(k), T.iq[:, :], start=(k == 0), stop=(k == NP))
+    mm.then_inc(S.tm, 1)
+
+    ka, kb = N - 2, N - 1
     g.vector.wait_ge(S.tm, 1)
-    g.vector.tensor_copy(T.ms[:, :], T.pm[:, 0:D]).then_inc(S.mc, 1)
-    g.scalar.wait_ge(S.tp, 1)
-    g.scalar.activation(T.pf[:, :], T.pp[:, 0:R], ActivationFunctionType.Copy).then_inc(S.pc, 1)
+    g.vector.wait_ge(arr(ka), n_eng)
+    g.vector.tensor_tensor(T.asum[:, :], T.pa[:, 0:W], slotq(ka), AluOpType.add).then_inc(S.mc, 1)
+
+    g.tensor.wait_ge(arr(kb), n_eng)
+    g.tensor.matmul(T.pq[:, 0:R], slotq(kb, 0, D), slotq(kb, D, W), start=True, stop=False)
+    g.tensor.wait_ge(S.mc, 1)
+    g.tensor.matmul(T.pq[:, 0:R], T.asum[:, 0:D], T.asum[:, D:W], start=False, stop=False)
+    g.tensor.matmul(T.pq[:, 0:R], T.asum[:, 0:D], slotq(kb, D, W), start=False, stop=False)
+    g.tensor.matmul(T.pq[:, 0:R], slotq(kb, 0, D), T.asum[:, D:W], start=False, stop=True).then_inc(S.mm2, 1)
+
+    g.vector.wait_ge(S.mc, 1)
+    g.vector.wait_ge(arr(kb), n_eng)
+    g.vector.tensor_tensor(T.pf[:, :], T.asum[:, D:W], slotq(kb, D, W), AluOpType.add).then_inc(S.pc, 1)
     g.scalar.wait_ge(S.pc, 1)
     g.scalar.dma_start(T.p[:, :], T.pf[:, :]).then_inc(S.st, 16)
 
-    g.tensor.wait_ge(S.mc, 1)
-    g.tensor.wait_ge(S.pc, 1)
-    g.tensor.matmul(T.pq[:, 0:R], T.ms[:, :], T.pf[:, :], start=True, stop=True).then_inc(S.mm2, 1)
     g.vector.wait_ge(S.mm2, 1)
     g.vector.tensor_copy(T.q2s[:, :], T.pq[:, 0:R]).then_inc(S.q2c, 1)
     g.sync.wait_ge(S.q2c, 1)
     g.sync.dma_start(T.q2[:, :], T.q2s[:, :]).then_inc(S.st, 16)
 
-    g.wait_ge(S.sent, n_eng)
+    g.wait_ge(S.sent, 2 * n_eng)
     g.wait_ge(S.st, 32)

from concourse.bass import DstId, RemoteDMATransfer
from concourse.mybir import AluOpType, ActivationFunctionType

N = 7
D = 128
R = 32
W = D + R
NP = 4

SCRATCH = {
    "landp": ("sbuf", [128, (NP + 1) * D], "bfloat16"),
    "landq": ("sbuf", [128, (N - 1 - NP) * W], "bfloat16"),
    "snd": ("sbuf", [128, W], "bfloat16"),
    "iq": ("sbuf", [128, W], "bfloat16"),
    "ones": ("sbuf", [128, D], "bfloat16"),
    "asum": ("sbuf", [128, W], "bfloat16"),
    "pf": ("sbuf", [128, R], "bfloat16"),
    "q2s": ("sbuf", [128, R], "bfloat16"),
    "pa": ("psum", [128, 512], "float32"),
    "pj": ("psum", [128, 512], "float32"),
    "pq": ("psum", [128, 512], "float32"),
}
SEMAPHORES = ["ld", "ldm", "ldq", "on", "idy", "tj", "sj", "tm", "mc", "pc", "mm2", "q2c", "st", "sent"] + \
             ["a%d" % j for j in range(N)]


def rank_program(g, core, T, topo):
    r = T.rank_of(core)
    if r is None:
        return
    S = T.sem
    cores = T.cores

    def slotp(k):
        return T.landp[:, k * D:(k + 1) * D]

    def slotq(k, lo=0, hi=W):
        base = (k - NP - 1) * W
        return T.landq[:, base + lo:base + hi]

    def arr(k):
        return S["a%d" % ((r - k) % N)]

    g.sync.dma_start(slotp(0), T.mt[:, :]).then_inc(S.ld, 16)
    g.scalar.dma_start(T.iq[:, D:W], T.q[:, :]).then_inc(S.ldq, 16)
    g.sync.dma_start(T.snd[:, 0:D], T.m[:, :]).then_inc(S.ldm, 16)
    g.vector.memset(T.ones[:, :], 1.0).then_inc(S.on, 1)

    dsts = [cores[(r + k) % N] for k in range(1, N)]
    mask = topo.mask(core, dsts[0])
    ids = []
    for d in dsts:
        if not topo.may_write(core, d):
            raise ValueError("core %d may not write to core %d" % (core, d))
        mask &= topo.mask(core, d)
        rid, pid, _se = topo.addr(d)
        ids.append(DstId(rid=rid, pnc=pid))
    n_eng = bin(mask).count("1")

    g.wait_ge(S.ld, 16)
    g.remote_dma_fused(
        [RemoteDMATransfer(dst_ids=ids[0:NP], dma_engine_mask=mask, remote_sem=S["a%d" % r],
                           srcs=[slotp(0)], dsts=[slotp(k) for k in range(1, NP + 1)], alu_op=0)],
        local_sem=S.sent)

    g.wait_ge(S.on, 1)
    g.affine_select(T.iq[:, 0:D], T.ones[:, :], [[-1, D]], AluOpType.is_equal, 0.0, 0, 1).then_inc(S.idy, 1)

    g.tensor.wait_ge(S.ld, 16)
    g.tensor.wait_ge(S.ldq, 16)
    g.tensor.matmul(T.pj[:, 0:R], slotp(0), T.iq[:, D:W], start=True, stop=True).then_inc(S.tj, 1)
    g.scalar.wait_ge(S.tj, 1)
    g.scalar.activation(T.snd[:, D:W], T.pj[:, 0:R], ActivationFunctionType.Copy).then_inc(S.sj, 1)

    g.wait_ge(S.sj, 1)
    g.wait_ge(S.ldm, 16)
    g.remote_dma_fused(
        [RemoteDMATransfer(dst_ids=ids[NP:], dma_engine_mask=mask, remote_sem=S["a%d" % r],
                           srcs=[T.snd[:, :]], dsts=[slotq(k) for k in range(NP + 1, N)], alu_op=0)],
        local_sem=S.sent)

    g.tensor.wait_ge(S.idy, 1)
    for k in range(NP + 1):
        if k:
            g.tensor.wait_ge(arr(k), n_eng)
        mm = g.tensor.matmul(T.pa[:, 0:W], slotp(k), T.iq[:, :], start=(k == 0), stop=(k == NP))
    mm.then_inc(S.tm, 1)

    ka, kb = N - 2, N - 1
    g.vector.wait_ge(S.tm, 1)
    g.vector.wait_ge(arr(ka), n_eng)
    g.vector.tensor_tensor(T.asum[:, :], T.pa[:, 0:W], slotq(ka), AluOpType.add).then_inc(S.mc, 1)

    g.tensor.wait_ge(arr(kb), n_eng)
    g.tensor.matmul(T.pq[:, 0:R], slotq(kb, 0, D), slotq(kb, D, W), start=True, stop=False)
    g.tensor.wait_ge(S.mc, 1)
    g.tensor.matmul(T.pq[:, 0:R], T.asum[:, 0:D], T.asum[:, D:W], start=False, stop=False)
    g.tensor.matmul(T.pq[:, 0:R], T.asum[:, 0:D], slotq(kb, D, W), start=False, stop=False)
    g.tensor.matmul(T.pq[:, 0:R], slotq(kb, 0, D), T.asum[:, D:W], start=False, stop=True).then_inc(S.mm2, 1)

    g.vector.wait_ge(S.mc, 1)
    g.vector.wait_ge(arr(kb), n_eng)
    g.vector.tensor_tensor(T.pf[:, :], T.asum[:, D:W], slotq(kb, D, W), AluOpType.add).then_inc(S.pc, 1)
    g.scalar.wait_ge(S.pc, 1)
    g.scalar.dma_start(T.p[:, :], T.pf[:, :]).then_inc(S.st, 16)

    g.vector.wait_ge(S.mm2, 1)
    g.vector.tensor_copy(T.q2s[:, :], T.pq[:, 0:R]).then_inc(S.q2c, 1)
    g.sync.wait_ge(S.q2c, 1)
    g.sync.dma_start(T.q2[:, :], T.q2s[:, :]).then_inc(S.st, 16)

    g.wait_ge(S.sent, 2 * n_eng)
    g.wait_ge(S.st, 32)
